import numpy as np
import ml_dtypes


def mxq(x, axis, fmt="e4m3"):
    dtype, down = {"e4m3": (ml_dtypes.float8_e4m3fn, 7), "e5m2": (ml_dtypes.float8_e5m2, 14)}[fmt]
    v = np.moveaxis(np.asarray(x, np.float32).astype(ml_dtypes.bfloat16).astype(np.float64), axis, -1)
    blocks = v.reshape(v.shape[:-1] + (-1, 32))
    amax = np.abs(blocks).max(-1, keepdims=True)
    byte = np.maximum(np.where(amax > 0, np.frexp(amax)[1] - 1 + 127, 0) - down, 1)
    scale = np.exp2(byte - 127.0)
    codes = (blocks / scale).astype(np.float32).astype(dtype).astype(np.float64)
    return np.moveaxis((codes * scale).reshape(v.shape), -1, axis)


WIDE = False


def mx_kscale(k):
    if not WIDE:
        return np.ones(k)
    levels = np.array([10, -10, 5, -5, 0])
    if k % 512:
        return np.exp2(np.random.permutation(np.resize(levels, k // 32))).repeat(32)
    a = np.empty((k // 512, 16))
    for p in range(k // 512):
        a[p, :8] = np.random.permutation(np.resize(levels, 8))
        for g in range(8):
            far = levels[np.abs(levels - a[p, g]) >= 10]
            a[p, g + 8] = far[np.random.randint(len(far))]
    return np.exp2(a.ravel()).repeat(32)


def f64(x):
    return np.asarray(x).astype(np.float64)


def striped(idx):
    return np.tile(np.asarray(idx).reshape(-1, 16).T, (8, 1)).astype(np.uint16)


def unstriped(offs):
    return offs[:16].T.reshape(-1).astype(np.int64)


def striped8(idx):
    return np.asarray(idx).reshape(8, -1, 16).transpose(0, 2, 1).reshape(128, -1).astype(np.uint16)


def unstriped8(offs):
    return offs.reshape(8, 16, -1).transpose(0, 2, 1).reshape(8, -1).astype(np.int64)


def pick8(x, idx, run):
    r = np.arange(len(x))
    return x[r[:, None], idx[r % (8 * run) // run]]


E2M1 = np.array([0.0, 0.5, 1.0, 1.5, 2.0, 3.0, 4.0, 6.0, -0.0, -0.5, -1.0, -1.5, -2.0, -3.0, -4.0, -6.0])


def pack_weight(w, fmt):
    k, n = w.shape
    w = f64(np.asarray(w, np.float32).astype(ml_dtypes.bfloat16)).reshape(k // 32, 32, n)
    amax = np.abs(w).max(1)
    if fmt == "e4m3":
        byte = np.frexp(amax)[1] - 1 + 127 - 7
    else:
        mant, ex = np.frexp(amax / 6.0)
        byte = np.where(mant > 0.5, ex, ex - 1) + 127
    byte = np.clip(np.where(amax > 0, byte, 1), 1, 254)
    scaled = (w * np.exp2(127.0 - byte)[:, None, :]).reshape(k, n).astype(np.float32)
    by_word = np.ascontiguousarray(scaled.reshape(k // 512, 128, 4, n).transpose(0, 1, 3, 2))
    if fmt == "e4m3":
        words = by_word.astype(ml_dtypes.float8_e4m3fn).view(np.uint8)
    else:
        c = by_word.astype(ml_dtypes.float4_e2m1fn).view(np.uint8) & 0xF
        words = (c[..., 0::2] | (c[..., 1::2] << 4)).reshape(k // 512, 128, 2 * n)
    return np.ascontiguousarray(words), np.ascontiguousarray(byte.astype(np.uint8).reshape(k // 512, 16, n))


def unpack_weight(words, scales, fmt):
    g, _, n = scales.shape
    words = np.ascontiguousarray(words).reshape(g, 128, n, -1)
    if fmt == "e4m3":
        vals = words.view(ml_dtypes.float8_e4m3fn).astype(np.float64)
    else:
        nib = np.empty((g, 128, n, 4), np.uint8)
        nib[..., 0::2] = words & 0xF
        nib[..., 1::2] = words >> 4
        vals = E2M1[nib]
    vals = vals * np.repeat(np.exp2(scales.astype(np.float64) - 127.0), 8, axis=1)[..., None]
    return vals.transpose(0, 1, 3, 2).reshape(g * 512, n)


K, J, R, T, U, F, O, S, N, Z = 512, 512, 512, 1024, 1024, 1024, 128, 256, 256, 1024


def setup_inputs():
    n = np.random.standard_normal
    idx = np.stack([np.random.permutation(T)[:J] for _ in range(8)])
    idx2 = np.stack([np.random.permutation(U)[:J] for _ in range(8)])
    idx3 = np.stack([np.random.permutation(F)[:R] for _ in range(8)])
    idx4 = np.stack([np.random.permutation(J)[:S] for _ in range(8)])
    idx5 = np.stack([np.random.permutation(S)[:O] for _ in range(8)])
    idx6 = np.random.permutation(S)[:O]
    idx7 = np.random.permutation(Z)[:N]
    fk = mx_kscale(K)
    fr = mx_kscale(R)
    vsp = pack_weight(n((R, Z)) * 1 / np.sqrt(R) / fr[:, None], "e4m3")
    return {
        "ta": (np.random.randint(-7, 8, (K, T)).astype(np.float64)).astype(np.float32),
        "tb": (np.random.randint(-7, 8, (K, U)).astype(np.float64)).astype(np.float32),
        "ga": ((np.random.randint(8, 25, (K, 1)) / 64.0) * fk[:, None]).astype(np.float32),
        "gb": ((np.random.randint(8, 25, (K, 1)) / 64.0) * fk[:, None]).astype(np.float32),
        "ua": (np.random.randint(-7, 8, (K, F)).astype(np.float64)).astype(np.float32),
        "ha": ((np.random.randint(8, 25, (K, 1)) / 1024.0) / fk[:, None]).astype(np.float32),
        "sa": (np.random.uniform(0.5, 1.6, (R, 1)) * fr[:, None]).astype(np.float32),
        "sb": (np.random.uniform(0.5, 1.6, (R, 1))).astype(np.float32),
        "sd": (np.random.uniform(0.5, 1.6, (R, 1))).astype(np.float32),
        "vs_words": vsp[0],
        "vs_scales": vsp[1],
        "offs": striped8(idx),
        "offs2": striped8(idx2),
        "offs3": striped8(idx3),
        "offs4": striped8(idx4),
        "offs5": striped8(idx5),
        "offs6": striped(idx6),
        "offs7": striped(idx7),
    }


def reference(ta, tb, ga, gb, ua, ha, sa, sb, sd, vs_words, vs_scales, offs, offs2, offs3, offs4, offs5, offs6, offs7):
    idx = unstriped8(offs)
    idx2 = unstriped8(offs2)
    idx3 = unstriped8(offs3)
    idx4 = unstriped8(offs4)
    idx5 = unstriped8(offs5)
    idx6 = unstriped(offs6)
    idx7 = unstriped(offs7)
    vsu = unpack_weight(vs_words, vs_scales, "e4m3")
    xc = np.maximum(pick8(f64(ta), idx, 64) * f64(ga), pick8(f64(tb), idx2, 64) * f64(gb))
    wc = pick8(f64(ua), idx3, 64) * f64(ha)
    wcq = mxq(wc, 0, "e4m3")
    xcq = mxq(xc, 0, "e4m3")
    a = wcq.T @ xcq
    h1 = pick8(a, idx4, 64) * f64(sa)
    hid = np.abs(pick8(h1, idx5, 64) * f64(sb) - h1[:, idx6] * f64(sd))
    vsidx7g = vsu[:, idx7]
    hidq = mxq(hid, 0, "e4m3")
    y = vsidx7g.T @ hidq
    return y

@@ -1,0 +1,176 @@
+from contextlib import ExitStack
+
+import concourse.mybir as mybir
+
+F32 = mybir.dt.float32
+BF16 = mybir.dt.bfloat16
+I32 = mybir.dt.int32
+U32 = mybir.dt.uint32
+U16 = mybir.dt.uint16
+U8 = mybir.dt.uint8
+FP8X4 = mybir.dt.float8_e4m3fn_x4
+ALU = mybir.AluOpType
+COPY = mybir.ActivationFunctionType.Copy
+
+P = 128
+PACK = 4
+K, J, R, T, O, S, N, Z = 512, 512, 512, 1024, 128, 256, 256, 1024
+FLOPS = 2 * K * R * J + 2 * R * N * O
+
+
+def tile_picked_largercode_codes_one_chain_store_plain_kernel(
+    tc, ta, tb, ga, gb, ua, ha, sa, sb, sd, vs_words, vs_scales,
+    offs, offs2, offs3, offs4, offs5, offs6, offs7, out,
+):
+    nc = tc.nc
+    with ExitStack() as ctx:
+        lists = ctx.enter_context(tc.tile_pool(name="lists", bufs=1))
+        keep = ctx.enter_context(tc.tile_pool(name="keep", bufs=1))
+        psum = ctx.enter_context(tc.psum_pool(name="psum", bufs=1))
+
+        def load_list(src, name):
+            dst = lists.tile([P, src.shape[1]], U16, name=name)
+            nc.sync.dma_start(dst[:], src)
+            return dst
+
+        def load_steps(queue, src, name):
+            dst = keep.tile([P, PACK], F32, name=name)
+            queue.dma_start(dst[:], src.rearrange("(p t) o -> p (t o)", t=PACK))
+            return dst
+
+        def load_rows(src, t, name):
+            dst = keep.tile([P, T], F32, name=name, align_bytes=64)
+            nc.sync.dma_start(dst[:], src.rearrange("(p t) c -> p t c", t=PACK)[:, t, :])
+            return dst
+
+        scale_window = keep.tile([P, Z], U8, name="scale_window", align_bytes=64)
+        nc.vector.memset(scale_window[:].bitcast(I32), 0)
+
+        ga_t = load_steps(nc.scalar, ga, "ga_t")
+        gb_t = load_steps(nc.scalar, gb, "gb_t")
+        ha_t = load_steps(nc.gpsimd, ha, "ha_t")
+        sa_t = load_steps(nc.gpsimd, sa, "sa_t")
+        sb_t = load_steps(nc.gpsimd, sb, "sb_t")
+        sd_t = load_steps(nc.gpsimd, sd, "sd_t")
+
+        ta_rows, tb_rows, ua_rows = [], [], []
+        ta_rows.append(load_rows(ta, 0, "ta0"))
+        l1 = load_list(offs, "l1")
+        tb_rows.append(load_rows(tb, 0, "tb0"))
+        l2 = load_list(offs2, "l2")
+        for t in range(1, PACK):
+            ta_rows.append(load_rows(ta, t, "ta%d" % t))
+            tb_rows.append(load_rows(tb, t, "tb%d" % t))
+        l3 = load_list(offs3, "l3")
+        for t in range(PACK):
+            ua_rows.append(load_rows(ua, t, "ua%d" % t))
+        l4 = load_list(offs4, "l4")
+        l5 = load_list(offs5, "l5")
+        l6 = load_list(offs6, "l6")
+        l7 = load_list(offs7, "l7")
+        word_window = keep.tile([P, Z], I32, name="word_window", align_bytes=64)
+        nc.sync.dma_start(word_window[:], vs_words[0].rearrange("p n t -> p (n t)").bitcast(I32))
+        for q in range(4):
+            nc.sync.dma_start(
+                scale_window[32 * q : 32 * q + 4, :].bitcast(I32),
+                vs_scales[0, 4 * q : 4 * q + 4, :].bitcast(I32),
+            )
+
+        x_planes = keep.tile([P, PACK, J], BF16, name="x_planes", align_bytes=64)
+        for t in range(PACK):
+            xa = keep.tile([P, J], F32, name="xa%d" % t, align_bytes=64)
+            xb = keep.tile([P, J], F32, name="xb%d" % t, align_bytes=64)
+            nc.scalar.activation(out=xa[:], in_=ta_rows[t][:].indirect(l1[:]), func=COPY, scale=ga_t[:, t : t + 1])
+            nc.scalar.activation(out=xb[:], in_=tb_rows[t][:].indirect(l2[:]), func=COPY, scale=gb_t[:, t : t + 1])
+            nc.vector.tensor_tensor(out=x_planes[:, t, :], in0=xa[:], in1=xb[:], op=ALU.max)
+        x_grouped = keep.tile([P, J, PACK], BF16, name="x_grouped", align_bytes=64)
+        nc.vector.tensor_copy(
+            out=x_grouped[:].rearrange("p (c i) t -> p c t i", i=4),
+            in_=x_planes[:].rearrange("p t (c i) -> p c t i", i=4),
+        )
+        x_codes = keep.tile([P, J], U32, name="x_codes", align_bytes=64)
+        x_scales = keep.tile([P, J], U8, name="x_scales", align_bytes=64)
+        nc.vector.quantize_mx(
+            out=x_codes[:].bitcast(FP8X4), scales=x_scales[:], in_=x_grouped[:].rearrange("p j t -> p (j t)")
+        )
+
+        half = R // 2
+        w_lo = keep.tile([P, PACK, half], BF16, name="w_lo", align_bytes=64)
+        w_hi = keep.tile([P, PACK, half], BF16, name="w_hi", align_bytes=64)
+        w_halves = [w_lo, w_hi]
+        cols = half // 16
+        for t in range(PACK):
+            for h in range(2):
+                nc.scalar.activation(
+                    out=w_halves[h][:, t, :],
+                    in_=ua_rows[t][:].indirect(l3[:, h * cols : (h + 1) * cols]),
+                    func=COPY,
+                    scale=ha_t[:, t : t + 1],
+                )
+        w_grouped = [keep.tile([P, P, PACK], BF16, name="w_grouped%d" % u, align_bytes=64) for u in range(PACK)]
+        w_codes = [keep.tile([P, P], U32, name="w_codes%d" % u, align_bytes=64) for u in range(PACK)]
+        w_scales = [keep.tile([P, P], U8, name="w_scales%d" % u, align_bytes=64) for u in range(PACK)]
+        for h in range(2):
+            for u in range(PACK):
+                nc.vector.tensor_copy(
+                    out=w_grouped[u][:, 64 * h : 64 * h + 64, :],
+                    in_=w_halves[h][:].rearrange("p t (m u) -> p u m t", u=PACK)[:, u, :, :],
+                )
+        a_rows = [keep.tile([P, J], F32, name="a_rows%d" % u, align_bytes=64) for u in range(PACK)]
+        for u in range(PACK):
+            nc.vector.quantize_mx(
+                out=w_codes[u][:].bitcast(FP8X4), scales=w_scales[u][:], in_=w_grouped[u][:].rearrange("p m t -> p (m t)")
+            )
+        for u in range(PACK):
+            pieces = 2 if u == 0 else 1
+            width = J // pieces
+            for c in range(pieces):
+                js = slice(c * width, (c + 1) * width)
+                acc = psum.tile([P, width], F32, name="acc%d_%d" % (u, c))
+                nc.tensor.matmul_mx(
+                    out=acc[:], lhsT=w_codes[u][:].bitcast(FP8X4), lhsT_scale=w_scales[u][:],
+                    rhs=x_codes[:, js].bitcast(FP8X4), rhs_scale=x_scales[:, js], start=True, stop=True,
+                )
+                if u == 0:
+                    nc.scalar.copy(out=a_rows[u][:, js], in_=acc[:])
+                else:
+                    nc.vector.tensor_copy(out=a_rows[u][:, js], in_=acc[:])
+
+        hid = keep.tile([P, O, PACK], BF16, name="hid", align_bytes=64)
+        for u in range(PACK):
+            h1 = keep.tile([P, S], F32, name="h1_%d" % u, align_bytes=64)
+            own = keep.tile([P, O], F32, name="own%d" % u, align_bytes=64)
+            shared = keep.tile([P, O], F32, name="shared%d" % u, align_bytes=64)
+            diff = keep.tile([P, O], F32, name="diff%d" % u, align_bytes=64)
+            nc.scalar.activation(out=h1[:], in_=a_rows[u][:].indirect(l4[:]), func=COPY, scale=sa_t[:, u : u + 1])
+            nc.scalar.activation(out=own[:], in_=h1[:].indirect(l5[:]), func=COPY, scale=sb_t[:, u : u + 1])
+            nc.scalar.activation(out=shared[:], in_=h1[:].indirect(l6[:]), func=COPY, scale=sd_t[:, u : u + 1])
+            nc.vector.tensor_tensor(out=diff[:], in0=own[:], in1=shared[:], op=ALU.subtract)
+            nc.vector.scalar_tensor_tensor(
+                out=hid[:, :, u], in0=diff[:], scalar=-1.0, in1=diff[:], op0=ALU.mult, op1=ALU.max
+            )
+
+        v_codes = keep.tile([P, N], U32, name="v_codes", align_bytes=64)
+        v_scales = keep.tile([P, N], U8, name="v_scales", align_bytes=64)
+        nc.vector.tensor_copy(out=v_codes[:], in_=word_window[:].bitcast(U32).indirect(l7[:]))
+        nc.vector.tensor_copy(out=v_scales[:], in_=scale_window[:].indirect(l7[:]))
+
+        h_codes = keep.tile([P, O], U32, name="h_codes", align_bytes=64)
+        h_scales = keep.tile([P, O], U8, name="h_scales", align_bytes=64)
+        nc.vector.quantize_mx(
+            out=h_codes[:].bitcast(FP8X4), scales=h_scales[:], in_=hid[:].rearrange("p o t -> p (o t)")
+        )
+        for b in range(N // P):
+            ns = slice(b * P, (b + 1) * P)
+            y_acc = psum.tile([P, O], F32, name="y_acc%d" % b)
+            y = keep.tile([P, O], F32, name="y%d" % b, align_bytes=64)
+            nc.tensor.matmul_mx(
+                out=y_acc[:], lhsT=v_codes[:, ns].bitcast(FP8X4), lhsT_scale=v_scales[:, ns],
+                rhs=h_codes[:].bitcast(FP8X4), rhs_scale=h_scales[:], start=True, stop=True,
+            )
+            if b == 0:
+                nc.vector.tensor_copy(out=y[:], in_=y_acc[:])
+                nc.sync.dma_start(out[ns, :], y[:])
+            else:
+                nc.scalar.copy(out=y[:], in_=y_acc[:])
+                nc.scalar.dma_start(out[ns, :], y[:])

@@ -11,6 +11,7 @@ U8 = mybir.dt.uint8
 FP8X4 = mybir.dt.float8_e4m3fn_x4
 ALU = mybir.AluOpType
 COPY = mybir.ActivationFunctionType.Copy
+ABS = mybir.ActivationFunctionType.Abs
 
 P = 128
 PACK = 4
@@ -43,15 +44,11 @@ def tile_picked_largercode_codes_one_chain_store_plain_kernel(
             nc.sync.dma_start(dst[:], src.rearrange("(p t) c -> p t c", t=PACK)[:, t, :])
             return dst
 
-        scale_window = keep.tile([P, Z], U8, name="scale_window", align_bytes=64)
+        scale_window = keep.tile([P, Z], U8, name="scale_window", tag="scales_then_diff", align_bytes=64)
         nc.vector.memset(scale_window[:].bitcast(I32), 0)
 
         ga_t = load_steps(nc.scalar, ga, "ga_t")
         gb_t = load_steps(nc.scalar, gb, "gb_t")
-        ha_t = load_steps(nc.gpsimd, ha, "ha_t")
-        sa_t = load_steps(nc.gpsimd, sa, "sa_t")
-        sb_t = load_steps(nc.gpsimd, sb, "sb_t")
-        sd_t = load_steps(nc.gpsimd, sd, "sd_t")
 
         ta_rows, tb_rows, ua_rows = [], [], []
         ta_rows.append(load_rows(ta, 0, "ta0"))
@@ -62,19 +59,23 @@ def tile_picked_largercode_codes_one_chain_store_plain_kernel(
             ta_rows.append(load_rows(ta, t, "ta%d" % t))
             tb_rows.append(load_rows(tb, t, "tb%d" % t))
         l3 = load_list(offs3, "l3")
+        ha_t = load_steps(nc.sync, ha, "ha_t")
         for t in range(PACK):
             ua_rows.append(load_rows(ua, t, "ua%d" % t))
         l4 = load_list(offs4, "l4")
-        l5 = load_list(offs5, "l5")
-        l6 = load_list(offs6, "l6")
+        sa_t = load_steps(nc.sync, sa, "sa_t")
         l7 = load_list(offs7, "l7")
-        word_window = keep.tile([P, Z], I32, name="word_window", align_bytes=64)
+        word_window = keep.tile([P, Z], I32, name="word_window", tag="words_then_diff", align_bytes=64)
         nc.sync.dma_start(word_window[:], vs_words[0].rearrange("p n t -> p (n t)").bitcast(I32))
         for q in range(4):
             nc.sync.dma_start(
                 scale_window[32 * q : 32 * q + 4, :].bitcast(I32),
                 vs_scales[0, 4 * q : 4 * q + 4, :].bitcast(I32),
             )
+        l5 = load_list(offs5, "l5")
+        sb_t = load_steps(nc.sync, sb, "sb_t")
+        l6 = load_list(offs6, "l6")
+        sd_t = load_steps(nc.sync, sd, "sd_t")
 
         x_planes = keep.tile([P, PACK, J], BF16, name="x_planes", align_bytes=64)
         for t in range(PACK):
@@ -95,65 +96,105 @@ def tile_picked_largercode_codes_one_chain_store_plain_kernel(
         )
 
         half = R // 2
-        w_lo = keep.tile([P, PACK, half], BF16, name="w_lo", align_bytes=64)
-        w_hi = keep.tile([P, PACK, half], BF16, name="w_hi", align_bytes=64)
-        w_halves = [w_lo, w_hi]
         cols = half // 16
-        for t in range(PACK):
+        w_early = keep.tile([P, 2, R], BF16, name="w_early", align_bytes=64)
+        w_late = [keep.tile([P, 2, half], BF16, name="w_late%d" % h, align_bytes=64) for h in range(2)]
+        for t in range(2):
+            nc.scalar.activation(
+                out=w_early[:, t, :], in_=ua_rows[t][:].indirect(l3[:]), func=COPY, scale=ha_t[:, t : t + 1]
+            )
+        for t in range(2, PACK):
             for h in range(2):
                 nc.scalar.activation(
-                    out=w_halves[h][:, t, :],
+                    out=w_late[h][:, t - 2, :],
                     in_=ua_rows[t][:].indirect(l3[:, h * cols : (h + 1) * cols]),
                     func=COPY,
                     scale=ha_t[:, t : t + 1],
                 )
-        w_grouped = [keep.tile([P, P, PACK], BF16, name="w_grouped%d" % u, align_bytes=64) for u in range(PACK)]
-        w_codes = [keep.tile([P, P], U32, name="w_codes%d" % u, align_bytes=64) for u in range(PACK)]
-        w_scales = [keep.tile([P, P], U8, name="w_scales%d" % u, align_bytes=64) for u in range(PACK)]
-        for h in range(2):
-            for u in range(PACK):
-                nc.vector.tensor_copy(
-                    out=w_grouped[u][:, 64 * h : 64 * h + 64, :],
-                    in_=w_halves[h][:].rearrange("p t (m u) -> p u m t", u=PACK)[:, u, :, :],
-                )
-        a_rows = [keep.tile([P, J], F32, name="a_rows%d" % u, align_bytes=64) for u in range(PACK)]
-        for u in range(PACK):
-            nc.vector.quantize_mx(
-                out=w_codes[u][:].bitcast(FP8X4), scales=w_scales[u][:], in_=w_grouped[u][:].rearrange("p m t -> p (m t)")
+        groups = [range(0, 1), range(1, PACK)]
+        w_grouped, w_codes, w_scales = [], [], []
+        for g, us in enumerate(groups):
+            w_grouped.append(keep.tile([P, len(us), P, PACK], BF16, name="w_grouped%d" % g, align_bytes=64))
+            w_codes.append(
+                keep.tile([P, len(us) * P], U32, name="w_codes%d" % g, align_bytes=64)
             )
-        for u in range(PACK):
-            pieces = 2 if u == 0 else 1
-            width = J // pieces
-            for c in range(pieces):
-                js = slice(c * width, (c + 1) * width)
-                acc = psum.tile([P, width], F32, name="acc%d_%d" % (u, c))
-                nc.tensor.matmul_mx(
-                    out=acc[:], lhsT=w_codes[u][:].bitcast(FP8X4), lhsT_scale=w_scales[u][:],
-                    rhs=x_codes[:, js].bitcast(FP8X4), rhs_scale=x_scales[:, js], start=True, stop=True,
-                )
-                if u == 0:
-                    nc.scalar.copy(out=a_rows[u][:, js], in_=acc[:])
-                else:
-                    nc.vector.tensor_copy(out=a_rows[u][:, js], in_=acc[:])
+            w_scales.append(keep.tile([P, len(us) * P], U8, name="w_scales%d" % g, align_bytes=64))
 
-        hid = keep.tile([P, O, PACK], BF16, name="hid", align_bytes=64)
-        for u in range(PACK):
-            h1 = keep.tile([P, S], F32, name="h1_%d" % u, align_bytes=64)
-            own = keep.tile([P, O], F32, name="own%d" % u, align_bytes=64)
-            shared = keep.tile([P, O], F32, name="shared%d" % u, align_bytes=64)
-            diff = keep.tile([P, O], F32, name="diff%d" % u, align_bytes=64)
-            nc.scalar.activation(out=h1[:], in_=a_rows[u][:].indirect(l4[:]), func=COPY, scale=sa_t[:, u : u + 1])
-            nc.scalar.activation(out=own[:], in_=h1[:].indirect(l5[:]), func=COPY, scale=sb_t[:, u : u + 1])
-            nc.scalar.activation(out=shared[:], in_=h1[:].indirect(l6[:]), func=COPY, scale=sd_t[:, u : u + 1])
-            nc.vector.tensor_tensor(out=diff[:], in0=own[:], in1=shared[:], op=ALU.subtract)
-            nc.vector.scalar_tensor_tensor(
-                out=hid[:, :, u], in0=diff[:], scalar=-1.0, in1=diff[:], op0=ALU.mult, op1=ALU.max
+        def quantize(g, ms):
+            words = slice(ms.start, (len(groups[g]) - 1) * P + ms.stop)
+            nc.vector.quantize_mx(
+                out=w_codes[g][:, words].bitcast(FP8X4), scales=w_scales[g][:, words],
+                in_=w_grouped[g][:, :, ms, :].rearrange("p u m t -> p (u m t)"),
             )
+
+        def deal(copy, g, src, ms, ts):
+            us = groups[g]
+            copy(
+                out=w_grouped[g][:, :, ms, ts],
+                in_=src[:].rearrange("p t (m u) -> p u m t", u=PACK)[:, us.start : us.stop, :, :],
+            )
+
+        for g in range(2):
+            deal(nc.vector.tensor_copy, g, w_early, slice(0, P), slice(0, 2))
+        lo, hi = slice(0, P // 2), slice(P // 2, P)
+        for g in range(2):
+            deal(nc.vector.tensor_copy, g, w_late[0], lo, slice(2, PACK))
+        quantize(0, lo)
+        deal(nc.scalar.copy, 0, w_late[1], hi, slice(2, PACK))
+        quantize(0, hi)
+        deal(nc.vector.tensor_copy, 1, w_late[1], hi, slice(2, PACK))
+        quantize(1, slice(0, P))
+        a_rows = [keep.tile([P, J], F32, name="a_rows%d" % u, tag="a_rows_then_own%d" % u, align_bytes=64) for u in range(PACK)]
+        for g, us in enumerate(groups):
+            for u in us:
+                ms = slice((u - us.start) * P, (u - us.start + 1) * P)
+                cuts = [0, 256, 384, J] if u == 0 else [0, J]
+                for c in range(len(cuts) - 1):
+                    js = slice(cuts[c], cuts[c + 1])
+                    acc = psum.tile([P, cuts[c + 1] - cuts[c]], F32, name="acc%d_%d" % (u, c))
+                    nc.tensor.matmul_mx(
+                        out=acc[:], lhsT=w_codes[g][:, ms].bitcast(FP8X4), lhsT_scale=w_scales[g][:, ms],
+                        rhs=x_codes[:, js].bitcast(FP8X4), rhs_scale=x_scales[:, js], start=True, stop=True,
+                    )
+                    if u == 0 and c != 1:
+                        nc.scalar.copy(out=a_rows[u][:, js], in_=acc[:])
+                    else:
+                        nc.vector.tensor_copy(out=a_rows[u][:, js], in_=acc[:])
 
         v_codes = keep.tile([P, N], U32, name="v_codes", align_bytes=64)
         v_scales = keep.tile([P, N], U8, name="v_scales", align_bytes=64)
         nc.vector.tensor_copy(out=v_codes[:], in_=word_window[:].bitcast(U32).indirect(l7[:]))
         nc.vector.tensor_copy(out=v_scales[:], in_=scale_window[:].indirect(l7[:]))
+
+        hid = keep.tile([P, O, PACK], BF16, name="hid", align_bytes=64)
+        h1 = [keep.tile([P, S], F32, name="h1_%d" % u, align_bytes=64) for u in range(PACK)]
+        diff = [
+            keep.tile([P, 2, O], F32, name="diff%d" % v, tag=tag, align_bytes=64)
+            for v, tag in enumerate(["words_then_diff", "scales_then_diff"])
+        ]
+
+        def seats(u):
+            nc.scalar.activation(out=h1[u][:], in_=a_rows[u][:].indirect(l4[:]), func=COPY, scale=sa_t[:, u : u + 1])
+
+        def places(u):
+            own_tag = "a_rows_then_own%d" % ((u + 1) % PACK)
+            looks = keep.tile([P, 2, O], F32, name="looks%d" % u, tag=own_tag, align_bytes=64)
+            own, shared = looks[:, 0, :], looks[:, 1, :]
+            nc.scalar.activation(out=own, in_=h1[u][:].indirect(l5[:]), func=COPY, scale=sb_t[:, u : u + 1])
+            nc.scalar.activation(out=shared, in_=h1[u][:].indirect(l6[:]), func=COPY, scale=sd_t[:, u : u + 1])
+            nc.vector.tensor_tensor(out=diff[u // 2][:, u % 2, :], in0=own, in1=shared, op=ALU.subtract)
+
+        seats(0)
+        for u in range(1, PACK):
+            seats(u)
+            places(u - 1)
+            if u == 2:
+                pair = diff[0][:].rearrange("p t o -> p o t")
+                nc.vector.scalar_tensor_tensor(
+                    out=hid[:, :, 0:2], in0=pair, scalar=-1.0, in1=pair, op0=ALU.mult, op1=ALU.max
+                )
+        places(PACK - 1)
+        nc.scalar.activation(out=hid[:, :, 2:4], in_=diff[1][:].rearrange("p t o -> p o t"), func=ABS)
 
         h_codes = keep.tile([P, O], U32, name="h_codes", align_bytes=64)
         h_scales = keep.tile([P, O], U8, name="h_scales", align_bytes=64)

@@ -49,6 +49,10 @@ def tile_picked_largercode_codes_one_chain_store_plain_kernel(
 
         ga_t = load_steps(nc.scalar, ga, "ga_t")
         gb_t = load_steps(nc.scalar, gb, "gb_t")
+        warm_in = keep.tile([P, 1], F32, name="warm_in")
+        warm_out = keep.tile([P, 1], F32, name="warm_out")
+        nc.vector.memset(warm_in[:], 0.0)
+        nc.scalar.activation(out=warm_out[:], in_=warm_in[:], func=ABS)
 
         ta_rows, tb_rows, ua_rows = [], [], []
         ta_rows.append(load_rows(ta, 0, "ta0"))

@@ -48,22 +48,22 @@ def tile_picked_largercode_codes_one_chain_store_plain_kernel(
         nc.vector.memset(scale_window[:].bitcast(I32), 0)
 
         ga_t = load_steps(nc.scalar, ga, "ga_t")
-        gb_t = load_steps(nc.scalar, gb, "gb_t")
         warm_in = keep.tile([P, 1], F32, name="warm_in")
         warm_out = keep.tile([P, 1], F32, name="warm_out")
-        nc.vector.memset(warm_in[:], 0.0)
+        nc.gpsimd.memset(warm_in[:], 0.0)
         nc.scalar.activation(out=warm_out[:], in_=warm_in[:], func=ABS)
+        ha_t = load_steps(nc.gpsimd, ha, "ha_t")
 
         ta_rows, tb_rows, ua_rows = [], [], []
         ta_rows.append(load_rows(ta, 0, "ta0"))
         l1 = load_list(offs, "l1")
         tb_rows.append(load_rows(tb, 0, "tb0"))
         l2 = load_list(offs2, "l2")
+        gb_t = load_steps(nc.sync, gb, "gb_t")
         for t in range(1, PACK):
             ta_rows.append(load_rows(ta, t, "ta%d" % t))
             tb_rows.append(load_rows(tb, t, "tb%d" % t))
         l3 = load_list(offs3, "l3")
-        ha_t = load_steps(nc.sync, ha, "ha_t")
         for t in range(PACK):
             ua_rows.append(load_rows(ua, t, "ua%d" % t))
         l4 = load_list(offs4, "l4")
@@ -152,10 +152,10 @@ def tile_picked_largercode_codes_one_chain_store_plain_kernel(
         for g, us in enumerate(groups):
             for u in us:
                 ms = slice((u - us.start) * P, (u - us.start + 1) * P)
-                cuts = [0, 256, 384, J] if u == 0 else [0, J]
+                cuts = [[0, 256, 384, J], [0, 256, J], [0, J], [0, J]][u]
                 for c in range(len(cuts) - 1):
                     js = slice(cuts[c], cuts[c + 1])
-                    acc = psum.tile([P, cuts[c + 1] - cuts[c]], F32, name="acc%d_%d" % (u, c))
+                    acc = psum.tile([P, cuts[c + 1] - cuts[c]], F32, name="acc%d_%d" % (u, c), tag="acc%d_%d" % (u, c))
                     nc.tensor.matmul_mx(
                         out=acc[:], lhsT=w_codes[g][:, ms].bitcast(FP8X4), lhsT_scale=w_scales[g][:, ms],
                         rhs=x_codes[:, js].bitcast(FP8X4), rhs_scale=x_scales[:, js], start=True, stop=True,
@@ -177,6 +177,8 @@ def tile_picked_largercode_codes_one_chain_store_plain_kernel(
             for v, tag in enumerate(["words_then_diff", "scales_then_diff"])
         ]
 
+        o_halves = [slice(0, O // 2), slice(O // 2, O)]
+
         def seats(u):
             nc.scalar.activation(out=h1[u][:], in_=a_rows[u][:].indirect(l4[:]), func=COPY, scale=sa_t[:, u : u + 1])
 
@@ -186,7 +188,10 @@ def tile_picked_largercode_codes_one_chain_store_plain_kernel(
             own, shared = looks[:, 0, :], looks[:, 1, :]
             nc.scalar.activation(out=own, in_=h1[u][:].indirect(l5[:]), func=COPY, scale=sb_t[:, u : u + 1])
             nc.scalar.activation(out=shared, in_=h1[u][:].indirect(l6[:]), func=COPY, scale=sd_t[:, u : u + 1])
-            nc.vector.tensor_tensor(out=diff[u // 2][:, u % 2, :], in0=own, in1=shared, op=ALU.subtract)
+            for places_ in o_halves if u == PACK - 1 else [slice(0, O)]:
+                nc.vector.tensor_tensor(
+                    out=diff[u // 2][:, u % 2, places_], in0=own[:, places_], in1=shared[:, places_], op=ALU.subtract
+                )
 
         seats(0)
         for u in range(1, PACK):
@@ -198,16 +203,21 @@ def tile_picked_largercode_codes_one_chain_store_plain_kernel(
                     out=hid[:, :, 0:2], in0=pair, scalar=-1.0, in1=pair, op0=ALU.mult, op1=ALU.max
                 )
         places(PACK - 1)
-        nc.scalar.activation(out=hid[:, :, 2:4], in_=diff[1][:].rearrange("p t o -> p o t"), func=ABS)
+        for places_ in o_halves:
+            nc.scalar.activation(
+                out=hid[:, places_, 2:4], in_=diff[1][:].rearrange("p t o -> p o t")[:, places_, :], func=ABS
+            )
 
         h_codes = keep.tile([P, O], U32, name="h_codes", align_bytes=64)
         h_scales = keep.tile([P, O], U8, name="h_scales", align_bytes=64)
-        nc.vector.quantize_mx(
-            out=h_codes[:].bitcast(FP8X4), scales=h_scales[:], in_=hid[:].rearrange("p o t -> p (o t)")
-        )
+        for places_ in o_halves:
+            nc.vector.quantize_mx(
+                out=h_codes[:, places_].bitcast(FP8X4), scales=h_scales[:, places_],
+                in_=hid[:, places_, :].rearrange("p o t -> p (o t)"),
+            )
         for b in range(N // P):
             ns = slice(b * P, (b + 1) * P)
-            y_acc = psum.tile([P, O], F32, name="y_acc%d" % b)
+            y_acc = psum.tile([P, O], F32, name="y_acc%d" % b, tag="acc0_%d" % b)
             y = keep.tile([P, O], F32, name="y%d" % b, align_bytes=64)
             nc.tensor.matmul_mx(
                 out=y_acc[:], lhsT=v_codes[:, ns].bitcast(FP8X4), lhsT_scale=v_scales[:, ns],

@@ -102,19 +102,21 @@ def tile_picked_largercode_codes_one_chain_store_plain_kernel(
         half = R // 2
         cols = half // 16
         w_early = keep.tile([P, 2, R], BF16, name="w_early", align_bytes=64)
-        w_late = [keep.tile([P, 2, half], BF16, name="w_late%d" % h, align_bytes=64) for h in range(2)]
+        w_late_tile = keep.tile([P, 2 * R], BF16, name="w_late", align_bytes=64)
+        w_late_planes = w_late_tile[:].rearrange("p (t r) -> p t r", t=2)
+        w_late = [w_late_planes[:, :, h * half : (h + 1) * half] for h in range(2)]
         for t in range(2):
             nc.scalar.activation(
                 out=w_early[:, t, :], in_=ua_rows[t][:].indirect(l3[:]), func=COPY, scale=ha_t[:, t : t + 1]
             )
-        for t in range(2, PACK):
-            for h in range(2):
-                nc.scalar.activation(
-                    out=w_late[h][:, t - 2, :],
-                    in_=ua_rows[t][:].indirect(l3[:, h * cols : (h + 1) * cols]),
-                    func=COPY,
-                    scale=ha_t[:, t : t + 1],
-                )
+        nc.scalar.activation(out=w_late_tile[:, 0:R], in_=ua_rows[2][:].indirect(l3[:]), func=COPY, scale=ha_t[:, 2:3])
+        for h in range(2):
+            nc.scalar.activation(
+                out=w_late_tile[:, R + h * half : R + (h + 1) * half],
+                in_=ua_rows[3][:].indirect(l3[:, h * cols : (h + 1) * cols]),
+                func=COPY,
+                scale=ha_t[:, 3:4],
+            )
         groups = [range(0, 1), range(1, PACK)]
         w_grouped, w_codes, w_scales = [], [], []
         for g, us in enumerate(groups):
@@ -135,11 +137,11 @@ def tile_picked_largercode_codes_one_chain_store_plain_kernel(
             us = groups[g]
             copy(
                 out=w_grouped[g][:, :, ms, ts],
-                in_=src[:].rearrange("p t (m u) -> p u m t", u=PACK)[:, us.start : us.stop, :, :],
+                in_=src.rearrange("p t (m u) -> p u m t", u=PACK)[:, us.start : us.stop, :, :],
             )
 
         for g in range(2):
-            deal(nc.vector.tensor_copy, g, w_early, slice(0, P), slice(0, 2))
+            deal(nc.vector.tensor_copy, g, w_early[:], slice(0, P), slice(0, 2))
         lo, hi = slice(0, P // 2), slice(P // 2, P)
         for g in range(2):
             deal(nc.vector.tensor_copy, g, w_late[0], lo, slice(2, PACK))
@@ -170,14 +172,15 @@ def tile_picked_largercode_codes_one_chain_store_plain_kernel(
         nc.vector.tensor_copy(out=v_codes[:], in_=word_window[:].bitcast(U32).indirect(l7[:]))
         nc.vector.tensor_copy(out=v_scales[:], in_=scale_window[:].indirect(l7[:]))
 
-        hid = keep.tile([P, O, PACK], BF16, name="hid", align_bytes=64)
+        HO = O // 2
+        halves = [slice(0, HO), slice(HO, O)]
+        hid = [keep.tile([P, HO, PACK], BF16, name="hid%d" % h, align_bytes=64) for h in range(2)]
         h1 = [keep.tile([P, S], F32, name="h1_%d" % u, align_bytes=64) for u in range(PACK)]
-        diff = [
-            keep.tile([P, 2, O], F32, name="diff%d" % v, tag=tag, align_bytes=64)
-            for v, tag in enumerate(["words_then_diff", "scales_then_diff"])
+        diff_early = keep.tile([P, 2, O], F32, name="diff_early", tag="words_then_diff", align_bytes=64)
+        diff_late = [
+            keep.tile([P, 2, HO], F32, name="diff_late0", tag="scales_then_diff", align_bytes=64),
+            keep.tile([P, 2, HO], F32, name="diff_late1", align_bytes=64),
         ]
-
-        o_halves = [slice(0, O // 2), slice(O // 2, O)]
 
         def seats(u):
             nc.scalar.activation(out=h1[u][:], in_=a_rows[u][:].indirect(l4[:]), func=COPY, scale=sa_t[:, u : u + 1])
@@ -187,45 +190,50 @@ def tile_picked_largercode_codes_one_chain_store_plain_kernel(
             looks = keep.tile([P, 2, O], F32, name="looks%d" % u, tag=own_tag, align_bytes=64)
             own, shared = looks[:, 0, :], looks[:, 1, :]
             nc.scalar.activation(out=own, in_=h1[u][:].indirect(l5[:]), func=COPY, scale=sb_t[:, u : u + 1])
-            nc.scalar.activation(out=shared, in_=h1[u][:].indirect(l6[:]), func=COPY, scale=sd_t[:, u : u + 1])
-            for places_ in o_halves if u == PACK - 1 else [slice(0, O)]:
-                nc.vector.tensor_tensor(
-                    out=diff[u // 2][:, u % 2, places_], in0=own[:, places_], in1=shared[:, places_], op=ALU.subtract
-                )
+            if u < PACK - 1:
+                nc.scalar.activation(out=shared, in_=h1[u][:].indirect(l6[:]), func=COPY, scale=sd_t[:, u : u + 1])
+            if u < 2:
+                nc.vector.tensor_tensor(out=diff_early[:, u, :], in0=own, in1=shared, op=ALU.subtract)
+            else:
+                for h, part in enumerate(halves):
+                    if u == PACK - 1:
+                        nc.scalar.activation(
+                            out=shared[:, part], in_=h1[u][:].indirect(l6[:, part.start // 16 : part.stop // 16]),
+                            func=COPY, scale=sd_t[:, u : u + 1],
+                        )
+                    nc.vector.tensor_tensor(
+                        out=diff_late[h][:, u - 2, :], in0=own[:, part], in1=shared[:, part], op=ALU.subtract
+                    )
 
         seats(0)
         for u in range(1, PACK):
             seats(u)
             places(u - 1)
             if u == 2:
-                pair = diff[0][:].rearrange("p t o -> p o t")
-                nc.vector.scalar_tensor_tensor(
-                    out=hid[:, :, 0:2], in0=pair, scalar=-1.0, in1=pair, op0=ALU.mult, op1=ALU.max
-                )
+                for h, part in enumerate(halves):
+                    pair = diff_early[:].rearrange("p t o -> p o t")[:, part, :]
+                    nc.vector.scalar_tensor_tensor(
+                        out=hid[h][:, :, 0:2], in0=pair, scalar=-1.0, in1=pair, op0=ALU.mult, op1=ALU.max
+                    )
         places(PACK - 1)
-        for places_ in o_halves:
-            nc.scalar.activation(
-                out=hid[:, places_, 2:4], in_=diff[1][:].rearrange("p t o -> p o t")[:, places_, :], func=ABS
-            )
-
-        h_codes = keep.tile([P, O], U32, name="h_codes", align_bytes=64)
-        h_scales = keep.tile([P, O], U8, name="h_scales", align_bytes=64)
-        for places_ in o_halves:
+        y = [keep.tile([P, O], F32, name="y%d" % b, align_bytes=64) for b in range(N // P)]
+        banks = [["acc0_0", "acc0_1"], ["acc0_2", "acc1_0"]]
+        for h in range(2):
+            nc.scalar.activation(out=hid[h][:, :, 2:4], in_=diff_late[h][:].rearrange("p t o -> p o t"), func=ABS)
+        for h, part in enumerate(halves):
+            h_codes = keep.tile([P, HO], U32, name="h_codes%d" % h, align_bytes=64)
+            h_scales = keep.tile([P, HO], U8, name="h_scales%d" % h, align_bytes=64)
             nc.vector.quantize_mx(
-                out=h_codes[:, places_].bitcast(FP8X4), scales=h_scales[:, places_],
-                in_=hid[:, places_, :].rearrange("p o t -> p (o t)"),
+                out=h_codes[:].bitcast(FP8X4), scales=h_scales[:], in_=hid[h][:].rearrange("p o t -> p (o t)")
             )
-        for b in range(N // P):
-            ns = slice(b * P, (b + 1) * P)
-            y_acc = psum.tile([P, O], F32, name="y_acc%d" % b, tag="acc0_%d" % b)
-            y = keep.tile([P, O], F32, name="y%d" % b, align_bytes=64)
-            nc.tensor.matmul_mx(
-                out=y_acc[:], lhsT=v_codes[:, ns].bitcast(FP8X4), lhsT_scale=v_scales[:, ns],
-                rhs=h_codes[:].bitcast(FP8X4), rhs_scale=h_scales[:], start=True, stop=True,
-            )
-            if b == 0:
-                nc.vector.tensor_copy(out=y[:], in_=y_acc[:])
-                nc.sync.dma_start(out[ns, :], y[:])
-            else:
-                nc.scalar.copy(out=y[:], in_=y_acc[:])
-                nc.scalar.dma_start(out[ns, :], y[:])
+            for b in range(N // P):
+                ns = slice(b * P, (b + 1) * P)
+                y_acc = psum.tile([P, HO], F32, name="y_acc%d_%d" % (h, b), tag=banks[h][b])
+                nc.tensor.matmul_mx(
+                    out=y_acc[:], lhsT=v_codes[:, ns].bitcast(FP8X4), lhsT_scale=v_scales[:, ns],
+                    rhs=h_codes[:].bitcast(FP8X4), rhs_scale=h_scales[:], start=True, stop=True,
+                )
+                copy_out = nc.vector.tensor_copy if b == 0 else nc.scalar.copy
+                copy_out(out=y[b][:, part], in_=y_acc[:])
+        nc.sync.dma_start(out[0:P, :], y[0][:])
+        nc.scalar.dma_start(out[P:N, :], y[1][:])

from contextlib import ExitStack

import concourse.mybir as mybir

F32 = mybir.dt.float32
BF16 = mybir.dt.bfloat16
I32 = mybir.dt.int32
U32 = mybir.dt.uint32
U16 = mybir.dt.uint16
U8 = mybir.dt.uint8
FP8X4 = mybir.dt.float8_e4m3fn_x4
ALU = mybir.AluOpType
COPY = mybir.ActivationFunctionType.Copy
ABS = mybir.ActivationFunctionType.Abs

P = 128
PACK = 4
K, J, R, T, O, S, N, Z = 512, 512, 512, 1024, 128, 256, 256, 1024
FLOPS = 2 * K * R * J + 2 * R * N * O


def tile_picked_largercode_codes_one_chain_store_plain_kernel(
    tc, ta, tb, ga, gb, ua, ha, sa, sb, sd, vs_words, vs_scales,
    offs, offs2, offs3, offs4, offs5, offs6, offs7, out,
):
    nc = tc.nc
    with ExitStack() as ctx:
        lists = ctx.enter_context(tc.tile_pool(name="lists", bufs=1))
        keep = ctx.enter_context(tc.tile_pool(name="keep", bufs=1))
        psum = ctx.enter_context(tc.psum_pool(name="psum", bufs=1))

        def load_list(src, name):
            dst = lists.tile([P, src.shape[1]], U16, name=name)
            nc.sync.dma_start(dst[:], src)
            return dst

        def load_steps(queue, src, name):
            dst = keep.tile([P, PACK], F32, name=name)
            queue.dma_start(dst[:], src.rearrange("(p t) o -> p (t o)", t=PACK))
            return dst

        def load_rows(src, t, name):
            dst = keep.tile([P, T], F32, name=name, align_bytes=64)
            nc.sync.dma_start(dst[:], src.rearrange("(p t) c -> p t c", t=PACK)[:, t, :])
            return dst

        scale_window = keep.tile([P, Z], U8, name="scale_window", tag="scales_then_diff", align_bytes=64)
        nc.vector.memset(scale_window[:].bitcast(I32), 0)

        ga_t = load_steps(nc.scalar, ga, "ga_t")
        warm_in = keep.tile([P, 1], F32, name="warm_in")
        warm_out = keep.tile([P, 1], F32, name="warm_out")
        nc.gpsimd.memset(warm_in[:], 0.0)
        nc.scalar.activation(out=warm_out[:], in_=warm_in[:], func=ABS)
        ha_t = load_steps(nc.gpsimd, ha, "ha_t")

        ta_rows, tb_rows, ua_rows = [], [], []
        ta_rows.append(load_rows(ta, 0, "ta0"))
        l1 = load_list(offs, "l1")
        tb_rows.append(load_rows(tb, 0, "tb0"))
        l2 = load_list(offs2, "l2")
        gb_t = load_steps(nc.sync, gb, "gb_t")
        for t in range(1, PACK):
            ta_rows.append(load_rows(ta, t, "ta%d" % t))
            tb_rows.append(load_rows(tb, t, "tb%d" % t))
        l3 = load_list(offs3, "l3")
        for t in range(PACK):
            ua_rows.append(load_rows(ua, t, "ua%d" % t))
        l4 = load_list(offs4, "l4")
        sa_t = load_steps(nc.sync, sa, "sa_t")
        l7 = load_list(offs7, "l7")
        word_window = keep.tile([P, Z], I32, name="word_window", tag="words_then_diff", align_bytes=64)
        nc.sync.dma_start(word_window[:], vs_words[0].rearrange("p n t -> p (n t)").bitcast(I32))
        for q in range(4):
            nc.sync.dma_start(
                scale_window[32 * q : 32 * q + 4, :].bitcast(I32),
                vs_scales[0, 4 * q : 4 * q + 4, :].bitcast(I32),
            )
        l5 = load_list(offs5, "l5")
        sb_t = load_steps(nc.sync, sb, "sb_t")
        l6 = load_list(offs6, "l6")
        sd_t = load_steps(nc.sync, sd, "sd_t")

        x_planes = keep.tile([P, PACK, J], BF16, name="x_planes", align_bytes=64)
        for t in range(PACK):
            xa = keep.tile([P, J], F32, name="xa%d" % t, align_bytes=64)
            xb = keep.tile([P, J], F32, name="xb%d" % t, align_bytes=64)
            nc.scalar.activation(out=xa[:], in_=ta_rows[t][:].indirect(l1[:]), func=COPY, scale=ga_t[:, t : t + 1])
            nc.scalar.activation(out=xb[:], in_=tb_rows[t][:].indirect(l2[:]), func=COPY, scale=gb_t[:, t : t + 1])
            nc.vector.tensor_tensor(out=x_planes[:, t, :], in0=xa[:], in1=xb[:], op=ALU.max)
        x_grouped = keep.tile([P, J, PACK], BF16, name="x_grouped", align_bytes=64)
        nc.vector.tensor_copy(
            out=x_grouped[:].rearrange("p (c i) t -> p c t i", i=4),
            in_=x_planes[:].rearrange("p t (c i) -> p c t i", i=4),
        )
        x_codes = keep.tile([P, J], U32, name="x_codes", align_bytes=64)
        x_scales = keep.tile([P, J], U8, name="x_scales", align_bytes=64)
        nc.vector.quantize_mx(
            out=x_codes[:].bitcast(FP8X4), scales=x_scales[:], in_=x_grouped[:].rearrange("p j t -> p (j t)")
        )

        half = R // 2
        cols = half // 16
        w_early = keep.tile([P, 2, R], BF16, name="w_early", align_bytes=64)
        w_late_tile = keep.tile([P, 2 * R], BF16, name="w_late", align_bytes=64)
        w_late_planes = w_late_tile[:].rearrange("p (t r) -> p t r", t=2)
        w_late = [w_late_planes[:, :, h * half : (h + 1) * half] for h in range(2)]
        for t in range(2):
            nc.scalar.activation(
                out=w_early[:, t, :], in_=ua_rows[t][:].indirect(l3[:]), func=COPY, scale=ha_t[:, t : t + 1]
            )
        nc.scalar.activation(out=w_late_tile[:, 0:R], in_=ua_rows[2][:].indirect(l3[:]), func=COPY, scale=ha_t[:, 2:3])
        for h in range(2):
            nc.scalar.activation(
                out=w_late_tile[:, R + h * half : R + (h + 1) * half],
                in_=ua_rows[3][:].indirect(l3[:, h * cols : (h + 1) * cols]),
                func=COPY,
                scale=ha_t[:, 3:4],
            )
        groups = [range(0, 1), range(1, PACK)]
        w_grouped, w_codes, w_scales = [], [], []
        for g, us in enumerate(groups):
            w_grouped.append(keep.tile([P, len(us), P, PACK], BF16, name="w_grouped%d" % g, align_bytes=64))
            w_codes.append(
                keep.tile([P, len(us) * P], U32, name="w_codes%d" % g, align_bytes=64)
            )
            w_scales.append(keep.tile([P, len(us) * P], U8, name="w_scales%d" % g, align_bytes=64))

        def quantize(g, ms):
            words = slice(ms.start, (len(groups[g]) - 1) * P + ms.stop)
            nc.vector.quantize_mx(
                out=w_codes[g][:, words].bitcast(FP8X4), scales=w_scales[g][:, words],
                in_=w_grouped[g][:, :, ms, :].rearrange("p u m t -> p (u m t)"),
            )

        def deal(copy, g, src, ms, ts):
            us = groups[g]
            copy(
                out=w_grouped[g][:, :, ms, ts],
                in_=src.rearrange("p t (m u) -> p u m t", u=PACK)[:, us.start : us.stop, :, :],
            )

        for g in range(2):
            deal(nc.vector.tensor_copy, g, w_early[:], slice(0, P), slice(0, 2))
        lo, hi = slice(0, P // 2), slice(P // 2, P)
        for g in range(2):
            deal(nc.vector.tensor_copy, g, w_late[0], lo, slice(2, PACK))
        quantize(0, lo)
        deal(nc.scalar.copy, 0, w_late[1], hi, slice(2, PACK))
        quantize(0, hi)
        deal(nc.vector.tensor_copy, 1, w_late[1], hi, slice(2, PACK))
        quantize(1, slice(0, P))
        a_rows = [keep.tile([P, J], F32, name="a_rows%d" % u, tag="a_rows_then_own%d" % u, align_bytes=64) for u in range(PACK)]
        for g, us in enumerate(groups):
            for u in us:
                ms = slice((u - us.start) * P, (u - us.start + 1) * P)
                cuts = [[0, 256, 384, J], [0, 256, J], [0, J], [0, J]][u]
                for c in range(len(cuts) - 1):
                    js = slice(cuts[c], cuts[c + 1])
                    acc = psum.tile([P, cuts[c + 1] - cuts[c]], F32, name="acc%d_%d" % (u, c), tag="acc%d_%d" % (u, c))
                    nc.tensor.matmul_mx(
                        out=acc[:], lhsT=w_codes[g][:, ms].bitcast(FP8X4), lhsT_scale=w_scales[g][:, ms],
                        rhs=x_codes[:, js].bitcast(FP8X4), rhs_scale=x_scales[:, js], start=True, stop=True,
                    )
                    if u == 0 and c != 1:
                        nc.scalar.copy(out=a_rows[u][:, js], in_=acc[:])
                    else:
                        nc.vector.tensor_copy(out=a_rows[u][:, js], in_=acc[:])

        v_codes = keep.tile([P, N], U32, name="v_codes", align_bytes=64)
        v_scales = keep.tile([P, N], U8, name="v_scales", align_bytes=64)
        nc.vector.tensor_copy(out=v_codes[:], in_=word_window[:].bitcast(U32).indirect(l7[:]))
        nc.vector.tensor_copy(out=v_scales[:], in_=scale_window[:].indirect(l7[:]))

        HO = O // 2
        halves = [slice(0, HO), slice(HO, O)]
        hid = [keep.tile([P, HO, PACK], BF16, name="hid%d" % h, align_bytes=64) for h in range(2)]
        h1 = [keep.tile([P, S], F32, name="h1_%d" % u, align_bytes=64) for u in range(PACK)]
        diff_early = keep.tile([P, 2, O], F32, name="diff_early", tag="words_then_diff", align_bytes=64)
        diff_late = [
            keep.tile([P, 2, HO], F32, name="diff_late0", tag="scales_then_diff", align_bytes=64),
            keep.tile([P, 2, HO], F32, name="diff_late1", align_bytes=64),
        ]

        def seats(u):
            nc.scalar.activation(out=h1[u][:], in_=a_rows[u][:].indirect(l4[:]), func=COPY, scale=sa_t[:, u : u + 1])

        def places(u):
            own_tag = "a_rows_then_own%d" % ((u + 1) % PACK)
            looks = keep.tile([P, 2, O], F32, name="looks%d" % u, tag=own_tag, align_bytes=64)
            own, shared = looks[:, 0, :], looks[:, 1, :]
            nc.scalar.activation(out=own, in_=h1[u][:].indirect(l5[:]), func=COPY, scale=sb_t[:, u : u + 1])
            if u < PACK - 1:
                nc.scalar.activation(out=shared, in_=h1[u][:].indirect(l6[:]), func=COPY, scale=sd_t[:, u : u + 1])
            if u < 2:
                nc.vector.tensor_tensor(out=diff_early[:, u, :], in0=own, in1=shared, op=ALU.subtract)
            else:
                for h, part in enumerate(halves):
                    if u == PACK - 1:
                        nc.scalar.activation(
                            out=shared[:, part], in_=h1[u][:].indirect(l6[:, part.start // 16 : part.stop // 16]),
                            func=COPY, scale=sd_t[:, u : u + 1],
                        )
                    nc.vector.tensor_tensor(
                        out=diff_late[h][:, u - 2, :], in0=own[:, part], in1=shared[:, part], op=ALU.subtract
                    )

        seats(0)
        for u in range(1, PACK):
            seats(u)
            places(u - 1)
            if u == 2:
                for h, part in enumerate(halves):
                    pair = diff_early[:].rearrange("p t o -> p o t")[:, part, :]
                    nc.vector.scalar_tensor_tensor(
                        out=hid[h][:, :, 0:2], in0=pair, scalar=-1.0, in1=pair, op0=ALU.mult, op1=ALU.max
                    )
        places(PACK - 1)
        y = [keep.tile([P, O], F32, name="y%d" % b, align_bytes=64) for b in range(N // P)]
        banks = [["acc0_0", "acc0_1"], ["acc0_2", "acc1_0"]]
        for h in range(2):
            nc.scalar.activation(out=hid[h][:, :, 2:4], in_=diff_late[h][:].rearrange("p t o -> p o t"), func=ABS)
        for h, part in enumerate(halves):
            h_codes = keep.tile([P, HO], U32, name="h_codes%d" % h, align_bytes=64)
            h_scales = keep.tile([P, HO], U8, name="h_scales%d" % h, align_bytes=64)
            nc.vector.quantize_mx(
                out=h_codes[:].bitcast(FP8X4), scales=h_scales[:], in_=hid[h][:].rearrange("p o t -> p (o t)")
            )
            for b in range(N // P):
                ns = slice(b * P, (b + 1) * P)
                y_acc = psum.tile([P, HO], F32, name="y_acc%d_%d" % (h, b), tag=banks[h][b])
                nc.tensor.matmul_mx(
                    out=y_acc[:], lhsT=v_codes[:, ns].bitcast(FP8X4), lhsT_scale=v_scales[:, ns],
                    rhs=h_codes[:].bitcast(FP8X4), rhs_scale=h_scales[:], start=True, stop=True,
                )
                copy_out = nc.vector.tensor_copy if b == 0 else nc.scalar.copy
                copy_out(out=y[b][:, part], in_=y_acc[:])
        nc.sync.dma_start(out[0:P, :], y[0][:])
        nc.scalar.dma_start(out[P:N, :], y[1][:])
